import numpy as np
import ml_dtypes


def mxq(x, axis, fmt="e4m3"):
    dtype, down = {"e4m3": (ml_dtypes.float8_e4m3fn, 7), "e5m2": (ml_dtypes.float8_e5m2, 14)}[fmt]
    v = np.moveaxis(np.asarray(x, np.float32).astype(ml_dtypes.bfloat16).astype(np.float64), axis, -1)
    blocks = v.reshape(v.shape[:-1] + (-1, 32))
    amax = np.abs(blocks).max(-1, keepdims=True)
    byte = np.maximum(np.where(amax > 0, np.frexp(amax)[1] - 1 + 127, 0) - down, 1)
    scale = np.exp2(byte - 127.0)
    codes = (blocks / scale).astype(np.float32).astype(dtype).astype(np.float64)
    return np.moveaxis((codes * scale).reshape(v.shape), -1, axis)


WIDE = False


def mx_kscale(k):
    if not WIDE:
        return np.ones(k)
    levels = np.array([10, -10, 5, -5, 0])
    if k % 512:
        return np.exp2(np.random.permutation(np.resize(levels, k // 32))).repeat(32)
    a = np.empty((k // 512, 16))
    for p in range(k // 512):
        a[p, :8] = np.random.permutation(np.resize(levels, 8))
        for g in range(8):
            far = levels[np.abs(levels - a[p, g]) >= 10]
            a[p, g + 8] = far[np.random.randint(len(far))]
    return np.exp2(a.ravel()).repeat(32)


def f64(x):
    return np.asarray(x).astype(np.float64)


def striped(idx):
    return np.tile(idx.reshape(-1, 16).T, (8, 1)).astype(np.uint16)


def unstriped(offs):
    return offs[:16].T.reshape(-1).astype(np.int64)


def pack_weight(w):
    k, n = w.shape
    w = f64(np.asarray(w, np.float32).astype(ml_dtypes.bfloat16)).reshape(k // 32, 32, n)
    amax = np.abs(w).max(1)
    byte = np.clip(np.where(amax > 0, np.frexp(amax)[1] - 1 + 127 - 7, 1), 1, 254)
    scaled = (w * np.exp2(127.0 - byte)[:, None, :]).reshape(k, n).astype(np.float32)
    words = np.ascontiguousarray(scaled.reshape(k // 512, 128, 4, n).transpose(0, 1, 3, 2)).astype(ml_dtypes.float8_e4m3fn).view(np.uint8)
    return words, np.ascontiguousarray(byte.astype(np.uint8).reshape(k // 512, 16, n))


def unpack_weight(words, scales):
    g, p, n, _ = words.shape
    vals = np.ascontiguousarray(words).view(ml_dtypes.float8_e4m3fn).astype(np.float64) * np.repeat(np.exp2(scales.astype(np.float64) - 127.0), 8, axis=1)[..., None]
    return vals.transpose(0, 1, 3, 2).reshape(g * 512, n)


E2M1 = np.array([0.0, 0.5, 1.0, 1.5, 2.0, 3.0, 4.0, 6.0, -0.0, -0.5, -1.0, -1.5, -2.0, -3.0, -4.0, -6.0])


def pack_fp4(w):
    k, n = w.shape
    w = f64(np.asarray(w, np.float32).astype(ml_dtypes.bfloat16)).reshape(k // 32, 32, n)
    amax = np.abs(w).max(1)
    mant, ex = np.frexp(amax / 6.0)
    byte = np.clip(np.where(amax > 0, np.where(mant > 0.5, ex, ex - 1) + 127, 1), 1, 254)
    scaled = (w * np.exp2(127.0 - byte)[:, None, :]).reshape(k, n).astype(np.float32)
    c = np.ascontiguousarray(scaled.reshape(k // 512, 128, 4, n).transpose(0, 1, 3, 2)).astype(ml_dtypes.float4_e2m1fn).view(np.uint8) & 0xF
    words = (c[..., 0::2] | (c[..., 1::2] << 4)).reshape(k // 512, 128, 2 * n)
    return np.ascontiguousarray(words), np.ascontiguousarray(byte.astype(np.uint8).reshape(k // 512, 16, n))


def unpack_fp4(words, scales):
    g, _, n = scales.shape
    words = np.ascontiguousarray(words).reshape(g, 128, n, 2)
    nib = np.empty((g, 128, n, 4), np.uint8)
    nib[..., 0::2] = words & 0xF
    nib[..., 1::2] = words >> 4
    vals = E2M1[nib] * np.repeat(np.exp2(scales.astype(np.float64) - 127.0), 8, axis=1)[..., None]
    return vals.transpose(0, 1, 3, 2).reshape(g * 512, n)


K, T, S, N, H = 1024, 1024, 512, 128, 512


def setup_inputs():
    n = np.random.standard_normal
    s = mx_kscale(K)[:, None]
    u = mx_kscale(H)
    packed_xT = pack_weight(n((K, T)) * s)
    packed_w1 = pack_fp4(n((K, H)) / np.sqrt(K) / s)
    packed_w2 = pack_fp4(n((K, H)) / np.sqrt(K) / s)
    packed_w3 = pack_fp4(n((H, N)) / np.sqrt(H) / u[:, None])
    return {
        "x_words": packed_xT[0],
        "x_scales": packed_xT[1],
        "w1_words": packed_w1[0],
        "w1_scales": packed_w1[1],
        "w2_words": packed_w2[0],
        "w2_scales": packed_w2[1],
        "x1": (np.random.uniform(0.1, 0.9, (H, S))).astype(np.float32),
        "unit": (np.random.uniform(0.6, 1.4, (H, 1)) * u[:, None]).astype(np.float32),
        "w3_words": packed_w3[0],
        "w3_scales": packed_w3[1],
        "offs": striped(np.random.permutation(T)[:S]),
    }


def reference(x_words, x_scales, w1_words, w1_scales, w2_words, w2_scales, x1, unit, w3_words, w3_scales, offs):
    x2 = -1.0 * f64(x1) + 1.0
    xq = unpack_weight(x_words, x_scales)[:, unstriped(offs)]
    tau = unpack_fp4(w2_words, w2_scales).T @ xq
    tau1 = np.tanh(tau)
    gam = np.exp(-0.7 * tau1)
    den1 = f64(x1) + x2 * gam
    r1 = gam / den1
    gg2 = unpack_fp4(w1_words, w1_scales).T @ xq
    gam2 = np.exp(-0.7 * np.tanh(gg2))
    den2 = x2 + f64(x1) * gam2
    lga = ((x2) ** 2) * (tau1 * ((r1) ** 2) + gam2 / ((den2) ** 2))
    gex = (f64(x1) * x2) * ((tau1 * gam) / den1 + gam2 / den2)
    hid = f64(unit) * (np.exp(0.6 * lga) * f64(x1) + gex)
    return unpack_fp4(w3_words, w3_scales).T @ mxq(hid, 0, "e4m3")

import math
from contextlib import ExitStack

import concourse.mybir as mybir
from concourse.masks import make_identity

K, T, S, N, H = 1024, 1024, 512, 128, 512
FLOPS = 2 * (2 * K * H * S + H * N * S)

F32 = mybir.dt.float32
BF16 = mybir.dt.bfloat16
I32 = mybir.dt.int32
U32 = mybir.dt.uint32
U16 = mybir.dt.uint16
U8 = mybir.dt.uint8
FP8X4 = mybir.dt.float8_e4m3fn_x4
FP4X4 = mybir.dt.float4_e2m1fn_x4
ACT = mybir.ActivationFunctionType
ALU = mybir.AluOpType

P = 128
PACK = 4
PASSES = K // (P * PACK)
CHUNKS = S // P


def load_scales(queue, plane, scales):
    rows = scales.rearrange("o (q r) c -> r q o c", r=4)
    for r in range(4):
        queue.dma_start(out=plane[r:P:32, :, :].bitcast(I32), in_=rows[r].bitcast(I32))


def tile_picked_ynrtlg_act_p_kernel(
    tc, x_words, x_scales, w1_words, w1_scales, w2_words, w2_scales, x1, unit, w3_words, w3_scales, offs, out
):
    nc = tc.nc
    with ExitStack() as ctx:
        keep = ctx.enter_context(tc.tile_pool(name="keep", bufs=1))
        psum = ctx.enter_context(tc.psum_pool(name="psum", bufs=1))

        offsets = keep.tile([P, S // 16], U16, name="offsets")
        nc.sync.dma_start(offsets[:], offs)

        x_plane = keep.tile([P, PASSES, T], U8, name="x_plane", align_bytes=64)
        w2_plane = keep.tile([P, PASSES, H], U8, name="w2_plane", align_bytes=64)
        w1_plane = keep.tile([P, PASSES, H], U8, name="w1_plane", align_bytes=64)
        w3_plane = keep.tile([P, 1, N], U8, name="w3_plane", align_bytes=64)
        nc.gpsimd.memset(x_plane[:].bitcast(I32), 0)
        for plane in (w1_plane, w2_plane, w3_plane):
            nc.vector.memset(plane[:].bitcast(I32), 0)

        x1_rows = x1.rearrange("(p t) j -> p t j", t=PACK)
        pieces = ((0, 1), (1, 2), (2, 4))
        frac = [keep.tile([P, hi - lo, S], F32, name="frac%d" % lo) for lo, hi in pieces]
        where = [(n, t - lo) for n, (lo, hi) in enumerate(pieces) for t in range(lo, hi)]
        x_table = [keep.tile([P, T], U32, name="x_table%d" % o, align_bytes=64) for o in range(PASSES)]
        w2_codes = keep.tile([P, PASSES, 2 * H], U8, name="w2_codes", align_bytes=64)
        w1_codes = keep.tile([P, PASSES, 2 * H], U8, name="w1_codes", align_bytes=64)
        w3_codes = keep.tile([P, 2 * N], U8, name="w3_codes", align_bytes=64)
        unit_sb = keep.tile([P, PACK], F32, name="unit_sb")
        ident = keep.tile([P, P], F32, name="ident")

        load_scales(nc.gpsimd, w1_plane, w1_scales)
        make_identity(nc, ident[:])

        nc.sync.dma_start(out=frac[0][:], in_=x1_rows[:, 0:1, :])
        load_scales(nc.sync, x_plane, x_scales)
        nc.sync.dma_start(out=frac[1][:], in_=x1_rows[:, 1:2, :])
        nc.sync.dma_start(out=frac[2][:], in_=x1_rows[:, 2:4, :])
        nc.sync.dma_start(out=x_table[0][:].bitcast(I32), in_=x_words[0].rearrange("p c r -> p (c r)").bitcast(I32))
        nc.sync.dma_start(out=w2_codes[:].bitcast(I32), in_=w2_words.rearrange("o p c -> p o c").bitcast(I32))
        load_scales(nc.sync, w2_plane, w2_scales)
        nc.sync.dma_start(out=x_table[1][:].bitcast(I32), in_=x_words[1].rearrange("p c r -> p (c r)").bitcast(I32))
        nc.sync.dma_start(out=w1_codes[:].bitcast(I32), in_=w1_words.rearrange("o p c -> p o c").bitcast(I32))
        nc.sync.dma_start(out=unit_sb[:], in_=unit.rearrange("(p t) o -> p (t o)", t=PACK))
        nc.sync.dma_start(out=w3_codes[:].bitcast(I32), in_=w3_words[0].bitcast(I32))
        load_scales(nc.sync, w3_plane, w3_scales)

        logit = []
        for h, (lo, hi) in enumerate(pieces):
            ln_a = keep.tile([P, hi - lo, S], F32, name="ln_a%d" % h)
            ln_b = keep.tile([P, hi - lo, S], F32, name="ln_b%d" % h)
            nc.scalar.activation(out=ln_a[:], in_=frac[h][:], func=ACT.Ln)
            nc.scalar.activation(out=ln_b[:], in_=frac[h][:], func=ACT.Ln, scale=-1.0, bias=1.0)
            lg = keep.tile([P, hi - lo, S], F32, name="logit%d" % h)
            for cols in (slice(0, P), slice(P, S)) if hi == PACK else (slice(0, S),):
                nc.vector.tensor_tensor(out=lg[:, :, cols], in0=ln_a[:, :, cols], in1=ln_b[:, :, cols], op=ALU.subtract)
            logit.append(lg)

        half_unit = keep.tile([P, PACK], F32, name="half_unit")
        nc.gpsimd.tensor_scalar(out=half_unit[:], in0=unit_sb[:], scalar1=0.5, scalar2=0.0, op0=ALU.mult, op1=ALU.add)
        factor = keep.tile([P, PACK, S], F32, name="factor")
        for t in range(PACK):
            nc.gpsimd.tensor_scalar(
                out=factor[:, t, :], in0=frac[where[t][0]][:, where[t][1], :], scalar1=half_unit[:, t : t + 1], scalar2=0.0, op0=ALU.mult, op1=ALU.add
            )
        out_bank = psum.tile([P, S], F32, name="out_bank")

        st = [dict() for i in range(CHUNKS)]

        def fresh(i, key, shape, dtype):
            st[i][key] = keep.tile(shape, dtype, name="%s%d" % (key, i), align_bytes=64)
            return st[i][key]

        picked_scales = []
        for o in range(PASSES):
            sc = keep.tile([P, S], U8, name="picked_scales%d" % o, align_bytes=64)
            nc.vector.tensor_copy(out=sc[:], in_=x_plane[:, o, :].indirect(offsets[:]))
            picked_scales.append(sc)
        first_words, rest_words = [], []
        for group, lo, hi in ((first_words, 0, P), (rest_words, P, S)):
            for o in range(PASSES):
                words = keep.tile([P, hi - lo], U32, name="picked_words%d_%d" % (o, lo), align_bytes=64)
                nc.vector.tensor_copy(out=words[:], in_=x_table[o][:].indirect(offsets[:, lo // 16 : hi // 16]))
                group.append(words)

        def picked_words(i, o):
            return first_words[o][:] if i == 0 else rest_words[o][:, (i - 1) * P : i * P]

        def products(i):
            tanhs = fresh(i, "tanhs", [P, 3, H], F32)
            for slot, codes, plane, sign in ((0, w2_codes, w2_plane, 1.0), (1, w1_codes, w1_plane, -1.0)):
                bank = psum.tile([P, H], F32, name="prod%d_%d" % (slot, i), tag="prod%d" % slot, bufs=2 - slot)
                for o in range(PASSES):
                    nc.tensor.matmul_mx(
                        out=bank[:],
                        lhsT=picked_words(i, o).bitcast(FP8X4),
                        lhsT_scale=picked_scales[o][:, i * P : (i + 1) * P],
                        rhs=codes[:, o, :].bitcast(FP4X4),
                        rhs_scale=plane[:, o, :],
                        start=(o == 0),
                        stop=(o == PASSES - 1),
                    )
                nc.scalar.activation(
                    out=tanhs[:, slot, :].rearrange("p (t m) -> p t m", t=PACK),
                    in_=bank[:].rearrange("p (m t) -> p t m", t=PACK),
                    func=ACT.Tanh,
                    scale=sign,
                )
            bank = psum.tile([P, H], F32, name="logit_t%d" % i, tag="logit_t", bufs=1)
            for t in range(PACK):
                nc.tensor.transpose(bank[:, t * P : (t + 1) * P], logit[where[t][0]][:, where[t][1], i * P : (i + 1) * P], ident[:])
            st[i]["logit_t"] = bank

        def args(i, slots):
            tanhs = st[i]["tanhs"]
            n = slots.stop - slots.start
            nc.vector.scalar_tensor_tensor(
                out=st[i]["u"][:, slots, :],
                in0=tanhs[:, slots, :],
                scalar=0.7,
                in1=st[i]["logit_t"][:].unsqueeze(1).to_broadcast([P, n, H]),
                op0=ALU.mult,
                op1=ALU.add,
            )
            if slots.stop == 2:
                nc.scalar.activation(out=tanhs[:, 2, :], in_=tanhs[:, 1, :], func=ACT.Exp, scale=0.7)
            nc.scalar.activation(out=st[i]["ac"][:, slots, :], in_=st[i]["u"][:, slots, :], func=ACT.Tanh, scale=-0.5)

        def first_terms(i, slots):
            nc.vector.scalar_tensor_tensor(
                out=st[i]["ps"][:, slots, :],
                in0=st[i]["ac"][:, slots, :],
                scalar=1.0,
                in1=st[i]["tanhs"][:, 0:3:2, :][:, slots, :],
                op0=ALU.add,
                op1=ALU.mult,
            )

        def second_terms(i, slots, cols):
            nc.vector.scalar_tensor_tensor(
                out=st[i]["qs"][:, slots, cols],
                in0=st[i]["ac"][:, slots, cols],
                scalar=1.0,
                in1=st[i]["ps"][:, slots, cols],
                op0=ALU.add,
                op1=ALU.mult,
            )

        def activity(i, cols):
            nc.vector.tensor_tensor(out=st[i]["lga"][:, cols], in0=st[i]["qs"][:, 0, cols], in1=st[i]["qs"][:, 1, cols], op=ALU.add)
            nc.scalar.activation(out=st[i]["ex"][:, cols], in_=st[i]["lga"][:, cols], func=ACT.Exp, scale=0.15, bias=math.log(2.0))

        def total(i):
            bank = psum.tile([P, H], F32, name="total%d" % i, tag="total", bufs=3)
            terms = (st[i]["ps"][:, 0, :], st[i]["ps"][:, 1, :], st[i]["ex"][:])
            for n, term in enumerate(terms):
                for t in range(PACK):
                    nc.tensor.matmul(
                        bank[:, t * P : (t + 1) * P],
                        term[:, t * P : (t + 1) * P],
                        ident[:],
                        start=(n == 0 and t == 0),
                        stop=(n == len(terms) - 1 and t == PACK - 1),
                        is_transpose=True,
                    )
            st[i]["total"] = bank

        def hidden(i):
            hid = fresh(i, "hid", [P, PACK * P], BF16)
            nc.vector.tensor_tensor(
                out=hid[:].rearrange("p (c j t) -> p c t j", j=4, t=PACK),
                in0=st[i]["total"][:].rearrange("p (t c j) -> p c t j", t=PACK, j=4),
                in1=factor[:, :, i * P : (i + 1) * P].rearrange("p t (c j) -> p c t j", j=4),
                op=ALU.mult,
            )

        def finish(i):
            codes = fresh(i, "hw", [P, P], U32)
            sc = fresh(i, "hs", [P, P], U8)
            nc.vector.quantize_mx(out=codes[:].bitcast(FP8X4), scales=sc[:], in_=st[i]["hid"][:])
            cols = slice(i * P, (i + 1) * P)
            nc.tensor.matmul_mx(
                out=out_bank[:, cols],
                lhsT=w3_codes[:].bitcast(FP4X4),
                lhsT_scale=w3_plane[:, 0, :],
                rhs=codes[:].bitcast(FP8X4),
                rhs_scale=sc[:],
                start=True,
                stop=True,
            )
            res = fresh(i, "res", [P, P], F32)
            nc.scalar.copy(out=res[:], in_=out_bank[:, cols])
            nc.sync.dma_start(out=out[:, cols], in_=res[:])

        for i in range(CHUNKS):
            for key in ("u", "ac", "ps", "qs"):
                fresh(i, key, [P, 2, H], F32)
            for key in ("lga", "ex"):
                fresh(i, key, [P, H], F32)
        both, whole = slice(0, 2), slice(0, H)
        chains = (slice(0, 1), slice(1, 2))
        halves = (slice(0, H // 2), slice(H // 2, H))

        products(0)
        for chain in chains:
            args(0, chain)
        for chain in chains:
            first_terms(0, chain)
            second_terms(0, chain, whole)
        products(1)
        args(1, both)
        activity(0, whole)
        total(0)
        for i in range(1, CHUNKS):
            if i + 1 < CHUNKS:
                products(i + 1)
                args(i + 1, both)
            first_terms(i, both)
            for cols in halves if i == CHUNKS - 1 else (whole,):
                second_terms(i, both, cols)
                activity(i, cols)
            if i == CHUNKS - 1:
                hidden(0)
                finish(0)
            total(i)
        for i in range(1, CHUNKS):
            hidden(i)
            finish(i)
